import numpy as np, ml_dtypes
CORES = [12,28,44,60,3,19,35,51]
N = 8
import mx_ref
NC = 128
BF = ml_dtypes.bfloat16
def setup_inputs(rng):
    def f(*shape):
        return mx_ref.flush((rng.standard_normal(shape, dtype=np.float32) * np.exp2(rng.integers(-2, 3, shape[:-1] + (1,)))).astype(BF))
    return {"w": f(N, 128, N * 512), "x": f(N, 128, N * 4 * NC)}
def setup_inputs_blocks(rng):
    d = setup_inputs(rng)
    for k in ("w", "x"): d[k] = mx_ref.spread(d[k], rng, 2)
    return d
def setup_inputs_wide(rng):
    d = setup_inputs(rng)
    for k in ("w", "x"): d[k] = mx_ref.flush((d[k].astype(np.float32) * np.exp2(rng.integers(-8, 9, (N, 1, 1))).astype(np.float32)).astype(BF))
    return d
def setup_inputs_zeros(rng):
    d = setup_inputs(rng); v = d["x"].reshape(N, 128, -1, 4).copy()
    v[np.broadcast_to((rng.random((N, 1, v.shape[2], 1)) < 0.33), v.shape)] = 0
    d["x"] = v.reshape(d["x"].shape)
    return d
def reference(w, x):
    y = np.zeros((N, 128, NC), np.float32)
    for r in range(N):
        for j in range(N):
            p = mx_ref.matmul(mx_ref.quantize(w[r][:, 512 * j:512 * j + 512]), mx_ref.quantize(x[j][:, 4 * NC * r:4 * NC * r + 4 * NC]))
            y[r] = p if j == 0 else y[r] + p
    return {"y": y}

@@ -1,0 +1,177 @@
+from concourse.bass import DstId, RemoteDMATransfer
+from concourse.mybir import dt
+
+N = 8
+TW = 128
+TB = 512
+NSIM = 64
+
+SCRATCH = {
+    "xb": ("sbuf", [128, N * TB], "bfloat16"),
+    "wb": ("sbuf", [128, N * TB], "bfloat16"),
+    "xq": ("sbuf", [128, N * TW], "float8_e4m3fn_x4"),
+    "xs": ("sbuf", [128, N * TW], "uint8"),
+    "wq": ("sbuf", [128, N * TW], "float8_e4m3fn_x4"),
+    "ws": ("sbuf", [128, N * TW], "uint8"),
+    "lq": ("sbuf", [128, N * TW], "float8_e4m3fn_x4"),
+    "ls": ("sbuf", [128, N * TW], "uint8"),
+    "ps": ("psum", [128, 512], "float32"),
+    "yb": ("sbuf", [128, 128], "float32"),
+}
+SEMAPHORES = ["l1", "l2", "l3", "lw1", "lw2", "q1", "q2", "q3", "v1", "v2", "gate", "fed", "snt",
+              "mm", "cp", "st"] + ["a%d" % j for j in range(N)]
+
+
+def _bits(m):
+    return [i for i in range(16) if (m >> i) & 1]
+
+
+def _mk(bs):
+    return sum(1 << b for b in bs)
+
+
+def _layout(r, T, topo):
+    me = T.cores[r]
+    ch = topo.chip(me)
+    near = [d for d in range(N) if d != r and topo.same_plane(ch, topo.chip(T.cores[d]))]
+    far = [d for d in range(N) if d != r and d not in near]
+    near.sort(key=lambda d: (d - r) % N)
+    pairs = [far[0:2], far[2:4]]
+    pairs.sort(key=lambda p: any(topo.mates(ch, topo.chip(T.cores[d])) for d in p))
+    hs = [h for h in range(NSIM) if h != me and topo.chip(h) == ch
+          and all(topo.may_write(h, T.cores[d]) for d in far)]
+    hs.sort(key=lambda h: (topo.die(h) != topo.die(me), h))
+    return near, far, pairs, hs[:3]
+
+
+def _direct_masks(r, T, topo):
+    near = _layout(r, T, topo)[0]
+    off = _bits(topo.mask(T.cores[r], T.cores[near[0]]))
+    q = len(off) // 4
+    cm = [off[0:2 * q], off[2 * q:3 * q], off[3 * q:4 * q]]
+    sm = [off[2 * q:4 * q], off[0:q], off[q:2 * q]]
+    return {d: (cm[i], sm[i]) for i, d in enumerate(near)}
+
+
+def _send(g, T, topo, items, local_sem):
+    trs = []
+    for dst_core, dst, src, eng, sem in items:
+        rid, pid, _ = topo.addr(dst_core)
+        trs.append(RemoteDMATransfer(dst_ids=[DstId(rid=rid, pnc=pid)], dma_engine_mask=_mk(eng),
+                                     remote_sem=sem, src=src, dst=dst))
+    g.remote_dma_fused(trs, local_sem=local_sem)
+    return sum(len(it[3]) for it in items)
+
+
+def _helper(g, core, T, topo):
+    S = T.sem
+    own = [r for r in range(N) if topo.chip(T.cores[r]) == topo.chip(core)]
+    if not own:
+        return
+    r = own[0]
+    near, far, pairs, hs = _layout(r, T, topo)
+    if core not in hs:
+        return
+    k = hs.index(core)
+    nfeed = len(_feed_engines(r, T, topo))
+    todo = pairs[k] if k < 2 else far
+    off = _bits(topo.mask(core, T.cores[far[0]]))
+    per = len(off) // len(todo)
+    items = []
+    for i, d in enumerate(todo):
+        eng = off[i * per:(i + 1) * per]
+        if k < 2:
+            items.append((T.cores[d], T.lq[:, r * TW:(r + 1) * TW].bitcast(dt.uint8),
+                          T.xq[:, d * TW:(d + 1) * TW].bitcast(dt.uint8), eng, S["a%d" % r]))
+        else:
+            items.append((T.cores[d], T.ls[:, r * TW:(r + 1) * TW], T.xs[:, d * TW:(d + 1) * TW], eng, S["a%d" % r]))
+    g.wait_ge(S.fed, nfeed)
+    n = _send(g, T, topo, items, S.snt)
+    g.wait_ge(S.snt, n)
+
+
+def _feed_engines(r, T, topo):
+    near, far, pairs, hs = _layout(r, T, topo)
+    me = T.cores[r]
+    off = _bits(topo.mask(me, T.cores[near[0]]))
+    return [b for b in _bits(topo.mask(me, hs[0])) if b not in off]
+
+
+def _far_count(j, r, T, topo):
+    near, far, pairs, hs = _layout(j, T, topo)
+    noff = len(_bits(topo.mask(hs[0], T.cores[r])))
+    return noff // 2 + noff // len(far)
+
+
+def rank_program(g, core, T, topo):
+    r = T.rank_of(core)
+    if r is None:
+        _helper(g, core, T, topo)
+        return
+    S = T.sem
+    sy, sc, ve, te = g.sync, g.scalar, g.vector, g.tensor
+    near, far, pairs, hs = _layout(r, T, topo)
+    p1, p2 = pairs
+    h0, f0 = min(near + [r]), min(far)
+
+    def bcol(d, n):
+        return slice(d * TB, (d + n) * TB)
+
+    def qcol(d, n):
+        return slice(d * TW, (d + n) * TW)
+
+    sy.dma_start(T.xb[:, bcol(p1[0], 2)], T.x[:, bcol(p1[0], 2)]).then_inc(S.l1, 16)
+    sy.dma_start(T.xb[:, bcol(p2[0], 2)], T.x[:, bcol(p2[0], 2)]).then_inc(S.l2, 16)
+    sy.dma_start(T.xb[:, bcol(h0, 4)], T.x[:, bcol(h0, 4)]).then_inc(S.l3, 16)
+    sy.dma_start(T.wb[:, bcol(h0, 4)], T.w[:, bcol(h0, 4)]).then_inc(S.lw1, 16)
+    sc.wait_ge(S.gate, 1)
+    sc.dma_start(T.wb[:, bcol(f0, 4)], T.w[:, bcol(f0, 4)]).then_inc(S.lw2, 16)
+
+    for lsem, qsem, q, s, b, d, n in ((S.l1, S.q1, T.xq, T.xs, T.xb, p1[0], 2), (S.l2, S.q2, T.xq, T.xs, T.xb, p2[0], 2),
+                                      (S.l3, S.q3, T.xq, T.xs, T.xb, h0, 4), (S.lw1, S.v1, T.wq, T.ws, T.wb, h0, 4),
+                                      (S.lw2, S.v2, T.wq, T.ws, T.wb, f0, 4)):
+        ve.wait_ge(lsem, 16)
+        ve.quantize_mx(q[:, qcol(d, n)], s[:, qcol(d, n)], b[:, bcol(d, n)]).then_inc(qsem, 1)
+
+    fe = _feed_engines(r, T, topo)
+    sent = 0
+    g.wait_ge(S.q1, 1)
+    sent += _send(g, T, topo, [(hs[0], T.xq[:, qcol(p1[0], 2)].bitcast(dt.uint8),
+                                T.xq[:, qcol(p1[0], 2)].bitcast(dt.uint8), fe, S.fed)], S.snt)
+    g.wait_ge(S.q2, 1)
+    sent += _send(g, T, topo, [(hs[1], T.xq[:, qcol(p2[0], 2)].bitcast(dt.uint8),
+                                T.xq[:, qcol(p2[0], 2)].bitcast(dt.uint8), fe, S.fed)], S.snt)
+    sent += _send(g, T, topo, [(hs[2], T.xs[:, qcol(f0, 4)], T.xs[:, qcol(f0, 4)], fe, S.fed)], S.snt)
+    g.sem_inc(S.gate, 1)
+    dm = _direct_masks(r, T, topo)
+    g.wait_ge(S.q3, 1)
+    sent += _send(g, T, topo, [(T.cores[d], T.lq[:, qcol(r, 1)].bitcast(dt.uint8),
+                                T.xq[:, qcol(d, 1)].bitcast(dt.uint8), dm[d][0], S["a%d" % r]) for d in near], S.snt)
+    sent += _send(g, T, topo, [(T.cores[d], T.ls[:, qcol(r, 1)], T.xs[:, qcol(d, 1)], dm[d][1], S["a%d" % r])
+                               for d in near], S.snt)
+
+    srcs = [r] + near + sorted(far, key=lambda j: _layout(j, T, topo)[2][1].count(r))
+    te.wait_ge(S.v1, 1)
+    te.wait_ge(S.q3, 1)
+    for i, j in enumerate(srcs):
+        if j == r:
+            xc, xp = T.xq[:, qcol(r, 1)], T.xs[:, qcol(r, 1)]
+        else:
+            if j in near:
+                m = _direct_masks(j, T, topo)[r]
+                cnt = len(m[0]) + len(m[1])
+            else:
+                cnt = _far_count(j, r, T, topo)
+                if j == srcs[1 + len(near)]:
+                    te.wait_ge(S.v2, 1)
+            te.wait_ge(S["a%d" % j], cnt)
+            xc, xp = T.lq[:, qcol(j, 1)], T.ls[:, qcol(j, 1)]
+        mmi = te.matmul_mx(T.ps[:, 0:128], T.wq[:, qcol(j, 1)], T.ws[:, qcol(j, 1)], xc, xp, i == 0, i == N - 1)
+    mmi.then_inc(S.mm, 1)
+
+    ve.wait_ge(S.mm, 1)
+    ve.tensor_copy(T.yb[:], T.ps[:, 0:128]).then_inc(S.cp, 1)
+    sy.wait_ge(S.cp, 1)
+    sy.dma_start(T.y[:, :], T.yb[:]).then_inc(S.st, 16)
+    sy.wait_ge(S.st, 16)
+    g.wait_ge(S.snt, sent)

@@ -18,7 +18,8 @@ SCRATCH = {
     "ps": ("psum", [128, 512], "float32"),
     "yb": ("sbuf", [128, 128], "float32"),
 }
-SEMAPHORES = ["l1", "l2", "l3", "lw1", "lw2", "q1", "q2", "q3", "v1", "v2", "gate", "fed", "snt",
+SEMAPHORES = ["l1", "l2", "l3", "l4", "lw1", "lw2", "lw3", "lw4", "q1", "q2", "q3", "q4",
+              "v1", "v2", "v3", "v4", "g1", "g2", "fed1", "fed2", "fed3", "snt",
               "mm", "cp", "st"] + ["a%d" % j for j in range(N)]
 
 
@@ -35,22 +36,35 @@ def _layout(r, T, topo):
     ch = topo.chip(me)
     near = [d for d in range(N) if d != r and topo.same_plane(ch, topo.chip(T.cores[d]))]
     far = [d for d in range(N) if d != r and d not in near]
-    near.sort(key=lambda d: (d - r) % N)
-    pairs = [far[0:2], far[2:4]]
-    pairs.sort(key=lambda p: any(topo.mates(ch, topo.chip(T.cores[d])) for d in p))
-    hs = [h for h in range(NSIM) if h != me and topo.chip(h) == ch
-          and all(topo.may_write(h, T.cores[d]) for d in far)]
-    hs.sort(key=lambda h: (topo.die(h) != topo.die(me), h))
-    return near, far, pairs, hs[:3]
+    half = sorted(near + [r])
+    hp = [half[0:2], half[2:4]]
+    ownp = [p for p in hp if r in p][0]
+    na = [p for p in hp if r not in p][0]
+    nb = [d for d in ownp if d != r][0]
+
+    def ismate(d):
+        return topo.mates(ch, topo.chip(T.cores[d]))
+
+    fp = sorted([far[0:2], far[2:4]], key=lambda p: any(ismate(d) for d in p))
+    cand = [h for h in range(NSIM) if h != me and topo.chip(h) == ch
+            and all(topo.may_write(h, T.cores[d]) for d in far)]
+    own = [h for h in cand if topo.die(h) == topo.die(me)]
+    oth = [h for h in cand if h not in own]
+    a = (own + oth)[0]
+    b = [h for h in oth + own if h != a][0]
+    return {"near": near, "far": far, "ownp": ownp, "na": na, "nb": nb, "p1": fp[0][::-1] if r % 2 else fp[0],
+            "p2": sorted(fp[1], key=ismate), "hs": [a, b]}
 
 
-def _direct_masks(r, T, topo):
-    near = _layout(r, T, topo)[0]
-    off = _bits(topo.mask(T.cores[r], T.cores[near[0]]))
-    q = len(off) // 4
-    cm = [off[0:2 * q], off[2 * q:3 * q], off[3 * q:4 * q]]
-    sm = [off[2 * q:4 * q], off[0:q], off[q:2 * q]]
-    return {d: (cm[i], sm[i]) for i, d in enumerate(near)}
+def _off(src, dst, topo):
+    return _bits(topo.mask(src, dst))
+
+
+def _feed_engines(r, T, topo):
+    lay = _layout(r, T, topo)
+    me = T.cores[r]
+    off = _off(me, T.cores[lay["near"][0]], topo)
+    return [b for b in _off(me, lay["hs"][0], topo) if b not in off]
 
 
 def _send(g, T, topo, items, local_sem):
@@ -63,44 +77,45 @@ def _send(g, T, topo, items, local_sem):
     return sum(len(it[3]) for it in items)
 
 
+def _qcol(d, n):
+    return slice(d * TW, (d + n) * TW)
+
+
 def _helper(g, core, T, topo):
     S = T.sem
     own = [r for r in range(N) if topo.chip(T.cores[r]) == topo.chip(core)]
     if not own:
         return
     r = own[0]
-    near, far, pairs, hs = _layout(r, T, topo)
-    if core not in hs:
+    lay = _layout(r, T, topo)
+    if core not in lay["hs"]:
         return
-    k = hs.index(core)
-    nfeed = len(_feed_engines(r, T, topo))
-    todo = pairs[k] if k < 2 else far
-    off = _bits(topo.mask(core, T.cores[far[0]]))
-    per = len(off) // len(todo)
+    k = lay["hs"].index(core)
+    hf = len(_feed_engines(r, T, topo)) // 2
+    arr = S["a%d" % r]
+    n = 0
+    for fed, pair in ((S.fed1, lay["p1"]), (S.fed2, lay["p2"])):
+        d = pair[k]
+        g.wait_ge(fed, hf)
+        n += _send(g, T, topo, [(T.cores[d], T.lq[:, _qcol(r, 1)].bitcast(dt.uint8),
+                                 T.xq[:, _qcol(d, 1)].bitcast(dt.uint8), _off(core, T.cores[d], topo), arr)], S.snt)
+    g.wait_ge(S.fed3, hf)
     items = []
-    for i, d in enumerate(todo):
-        eng = off[i * per:(i + 1) * per]
-        if k < 2:
-            items.append((T.cores[d], T.lq[:, r * TW:(r + 1) * TW].bitcast(dt.uint8),
-                          T.xq[:, d * TW:(d + 1) * TW].bitcast(dt.uint8), eng, S["a%d" % r]))
-        else:
-            items.append((T.cores[d], T.ls[:, r * TW:(r + 1) * TW], T.xs[:, d * TW:(d + 1) * TW], eng, S["a%d" % r]))
-    g.wait_ge(S.fed, nfeed)
-    n = _send(g, T, topo, items, S.snt)
+    for i, d in enumerate((lay["p1"], lay["p2"])[k]):
+        off = _off(core, T.cores[d], topo)
+        h = len(off) // 2
+        items.append((T.cores[d], T.ls[:, _qcol(r, 1)], T.xs[:, _qcol(d, 1)], off[i * h:(i + 1) * h], arr))
+    n += _send(g, T, topo, items, S.snt)
     g.wait_ge(S.snt, n)
 
 
-def _feed_engines(r, T, topo):
-    near, far, pairs, hs = _layout(r, T, topo)
-    me = T.cores[r]
-    off = _bits(topo.mask(me, T.cores[near[0]]))
-    return [b for b in _bits(topo.mask(me, hs[0])) if b not in off]
-
-
-def _far_count(j, r, T, topo):
-    near, far, pairs, hs = _layout(j, T, topo)
-    noff = len(_bits(topo.mask(hs[0], T.cores[r])))
-    return noff // 2 + noff // len(far)
+def _arrivals(j, r, T, topo):
+    lay = _layout(j, T, topo)
+    if r in lay["far"]:
+        noff = len(_off(lay["hs"][0], T.cores[r], topo))
+        return noff + noff // 2
+    noff = len(_off(T.cores[j], T.cores[r], topo))
+    return 2 * noff if r == lay["nb"] else 2 * (noff // 2)
 
 
 def rank_program(g, core, T, topo):
@@ -110,61 +125,68 @@ def rank_program(g, core, T, topo):
         return
     S = T.sem
     sy, sc, ve, te = g.sync, g.scalar, g.vector, g.tensor
-    near, far, pairs, hs = _layout(r, T, topo)
-    p1, p2 = pairs
-    h0, f0 = min(near + [r]), min(far)
+    lay = _layout(r, T, topo)
+    far, p1, p2, hs, na, nb, ownp = lay["far"], lay["p1"], lay["p2"], lay["hs"], lay["na"], lay["nb"], lay["ownp"]
+    h0 = min(na + ownp)
+    fa = [j for j in far if r in _layout(j, T, topo)["p1"]]
+    fb = sorted([j for j in far if r in _layout(j, T, topo)["p2"]], key=lambda j: -_layout(j, T, topo)["p2"].index(r))
 
     def bcol(d, n):
         return slice(d * TB, (d + n) * TB)
 
-    def qcol(d, n):
-        return slice(d * TW, (d + n) * TW)
+    qcol = _qcol
 
-    sy.dma_start(T.xb[:, bcol(p1[0], 2)], T.x[:, bcol(p1[0], 2)]).then_inc(S.l1, 16)
-    sy.dma_start(T.xb[:, bcol(p2[0], 2)], T.x[:, bcol(p2[0], 2)]).then_inc(S.l2, 16)
-    sy.dma_start(T.xb[:, bcol(h0, 4)], T.x[:, bcol(h0, 4)]).then_inc(S.l3, 16)
+    sy.dma_start(T.xb[:, bcol(min(p1), 2)], T.x[:, bcol(min(p1), 2)]).then_inc(S.l1, 16)
+    sy.dma_start(T.xb[:, bcol(min(p2), 2)], T.x[:, bcol(min(p2), 2)]).then_inc(S.l2, 16)
+    sy.dma_start(T.xb[:, bcol(min(na), 2)], T.x[:, bcol(min(na), 2)]).then_inc(S.l3, 16)
+    sy.dma_start(T.xb[:, bcol(min(ownp), 2)], T.x[:, bcol(min(ownp), 2)]).then_inc(S.l4, 16)
     sy.dma_start(T.wb[:, bcol(h0, 4)], T.w[:, bcol(h0, 4)]).then_inc(S.lw1, 16)
-    sc.wait_ge(S.gate, 1)
-    sc.dma_start(T.wb[:, bcol(f0, 4)], T.w[:, bcol(f0, 4)]).then_inc(S.lw2, 16)
+    sc.wait_ge(S.g1, 1)
+    sc.dma_start(T.wb[:, bcol(min(fa), 2)], T.w[:, bcol(min(fa), 2)]).then_inc(S.lw2, 16)
+    sc.wait_ge(S.g2, 1)
+    sc.dma_start(T.wb[:, bcol(fb[0], 1)], T.w[:, bcol(fb[0], 1)]).then_inc(S.lw3, 16)
+    sc.dma_start(T.wb[:, bcol(fb[1], 1)], T.w[:, bcol(fb[1], 1)]).then_inc(S.lw4, 16)
 
-    for lsem, qsem, q, s, b, d, n in ((S.l1, S.q1, T.xq, T.xs, T.xb, p1[0], 2), (S.l2, S.q2, T.xq, T.xs, T.xb, p2[0], 2),
-                                      (S.l3, S.q3, T.xq, T.xs, T.xb, h0, 4), (S.lw1, S.v1, T.wq, T.ws, T.wb, h0, 4),
-                                      (S.lw2, S.v2, T.wq, T.ws, T.wb, f0, 4)):
+    for lsem, qsem, q, s, b, d, n in ((S.l1, S.q1, T.xq, T.xs, T.xb, min(p1), 2), (S.l2, S.q2, T.xq, T.xs, T.xb, min(p2), 2),
+                                      (S.l3, S.q3, T.xq, T.xs, T.xb, min(na), 2), (S.l4, S.q4, T.xq, T.xs, T.xb, min(ownp), 2),
+                                      (S.lw1, S.v1, T.wq, T.ws, T.wb, h0, 4),
+                                      (S.lw2, S.v2, T.wq, T.ws, T.wb, min(fa), 2), (S.lw3, S.v3, T.wq, T.ws, T.wb, fb[0], 1),
+                                      (S.lw4, S.v4, T.wq, T.ws, T.wb, fb[1], 1)):
         ve.wait_ge(lsem, 16)
         ve.quantize_mx(q[:, qcol(d, n)], s[:, qcol(d, n)], b[:, bcol(d, n)]).then_inc(qsem, 1)
 
     fe = _feed_engines(r, T, topo)
+    hf = len(fe) // 2
+    arr = S["a%d" % r]
     sent = 0
-    g.wait_ge(S.q1, 1)
-    sent += _send(g, T, topo, [(hs[0], T.xq[:, qcol(p1[0], 2)].bitcast(dt.uint8),
-                                T.xq[:, qcol(p1[0], 2)].bitcast(dt.uint8), fe, S.fed)], S.snt)
-    g.wait_ge(S.q2, 1)
-    sent += _send(g, T, topo, [(hs[1], T.xq[:, qcol(p2[0], 2)].bitcast(dt.uint8),
-                                T.xq[:, qcol(p2[0], 2)].bitcast(dt.uint8), fe, S.fed)], S.snt)
-    sent += _send(g, T, topo, [(hs[2], T.xs[:, qcol(f0, 4)], T.xs[:, qcol(f0, 4)], fe, S.fed)], S.snt)
-    g.sem_inc(S.gate, 1)
-    dm = _direct_masks(r, T, topo)
+    for qsem, fed, pair in ((S.q1, S.fed1, p1), (S.q2, S.fed2, p2)):
+        g.wait_ge(qsem, 1)
+        sent += _send(g, T, topo, [(hs[i], T.xq[:, qcol(d, 1)].bitcast(dt.uint8), T.xq[:, qcol(d, 1)].bitcast(dt.uint8),
+                                    fe[i * hf:(i + 1) * hf], fed) for i, d in enumerate(pair)], S.snt)
+    sent += _send(g, T, topo, [(hs[i], T.xs[:, qcol(min(pair), 2)], T.xs[:, qcol(min(pair), 2)],
+                                fe[i * hf:(i + 1) * hf], S.fed3) for i, pair in enumerate((p1, p2))], S.snt)
+    g.sem_inc(S.g1, 1)
     g.wait_ge(S.q3, 1)
-    sent += _send(g, T, topo, [(T.cores[d], T.lq[:, qcol(r, 1)].bitcast(dt.uint8),
-                                T.xq[:, qcol(d, 1)].bitcast(dt.uint8), dm[d][0], S["a%d" % r]) for d in near], S.snt)
-    sent += _send(g, T, topo, [(T.cores[d], T.ls[:, qcol(r, 1)], T.xs[:, qcol(d, 1)], dm[d][1], S["a%d" % r])
-                               for d in near], S.snt)
+    off = _off(core, T.cores[na[0]], topo)
+    ho = len(off) // 2
+    sent += _send(g, T, topo, [(T.cores[d], T.lq[:, qcol(r, 1)].bitcast(dt.uint8), T.xq[:, qcol(d, 1)].bitcast(dt.uint8),
+                                off[i * ho:(i + 1) * ho], arr) for i, d in enumerate(na)], S.snt)
+    sent += _send(g, T, topo, [(T.cores[d], T.ls[:, qcol(r, 1)], T.xs[:, qcol(d, 1)],
+                                off[i * ho:(i + 1) * ho], arr) for i, d in enumerate(na)], S.snt)
+    g.sem_inc(S.g2, 1)
+    g.wait_ge(S.q4, 1)
+    sent += _send(g, T, topo, [(T.cores[nb], T.lq[:, qcol(r, 1)].bitcast(dt.uint8),
+                                T.xq[:, qcol(nb, 1)].bitcast(dt.uint8), off, arr)], S.snt)
+    sent += _send(g, T, topo, [(T.cores[nb], T.ls[:, qcol(r, 1)], T.xs[:, qcol(nb, 1)], off, arr)], S.snt)
 
-    srcs = [r] + near + sorted(far, key=lambda j: _layout(j, T, topo)[2][1].count(r))
-    te.wait_ge(S.v1, 1)
-    te.wait_ge(S.q3, 1)
-    for i, j in enumerate(srcs):
+    srcs = [(j, S.v1) for j in [r] + na] + [(j, S.v2) for j in fa] + [(nb, S.v1), (fb[0], S.v3), (fb[1], S.v4)]
+    for i, (j, vsem) in enumerate(srcs):
+        te.wait_ge(vsem, 1)
         if j == r:
+            te.wait_ge(S.q4, 1)
             xc, xp = T.xq[:, qcol(r, 1)], T.xs[:, qcol(r, 1)]
         else:
-            if j in near:
-                m = _direct_masks(j, T, topo)[r]
-                cnt = len(m[0]) + len(m[1])
-            else:
-                cnt = _far_count(j, r, T, topo)
-                if j == srcs[1 + len(near)]:
-                    te.wait_ge(S.v2, 1)
-            te.wait_ge(S["a%d" % j], cnt)
+            te.wait_ge(S["a%d" % j], _arrivals(j, r, T, topo))
             xc, xp = T.lq[:, qcol(j, 1)], T.ls[:, qcol(j, 1)]
         mmi = te.matmul_mx(T.ps[:, 0:128], T.wq[:, qcol(j, 1)], T.ws[:, qcol(j, 1)], xc, xp, i == 0, i == N - 1)
     mmi.then_inc(S.mm, 1)

from concourse.bass import DstId, RemoteDMATransfer
from concourse.mybir import dt

N = 8
TW = 128
TB = 512
NSIM = 64

SCRATCH = {
    "xb": ("sbuf", [128, N * TB], "bfloat16"),
    "wb": ("sbuf", [128, N * TB], "bfloat16"),
    "xq": ("sbuf", [128, N * TW], "float8_e4m3fn_x4"),
    "xs": ("sbuf", [128, N * TW], "uint8"),
    "wq": ("sbuf", [128, N * TW], "float8_e4m3fn_x4"),
    "ws": ("sbuf", [128, N * TW], "uint8"),
    "lq": ("sbuf", [128, N * TW], "float8_e4m3fn_x4"),
    "ls": ("sbuf", [128, N * TW], "uint8"),
    "ps": ("psum", [128, 512], "float32"),
    "yb": ("sbuf", [128, 128], "float32"),
}
SEMAPHORES = ["l1", "l2", "l3", "l4", "lw1", "lw2", "lw3", "lw4", "q1", "q2", "q3", "q4",
              "v1", "v2", "v3", "v4", "g1", "g2", "fed1", "fed2", "fed3", "snt",
              "mm", "cp", "st"] + ["a%d" % j for j in range(N)]


def _bits(m):
    return [i for i in range(16) if (m >> i) & 1]


def _mk(bs):
    return sum(1 << b for b in bs)


def _layout(r, T, topo):
    me = T.cores[r]
    ch = topo.chip(me)
    near = [d for d in range(N) if d != r and topo.same_plane(ch, topo.chip(T.cores[d]))]
    far = [d for d in range(N) if d != r and d not in near]
    half = sorted(near + [r])
    hp = [half[0:2], half[2:4]]
    ownp = [p for p in hp if r in p][0]
    na = [p for p in hp if r not in p][0]
    nb = [d for d in ownp if d != r][0]

    def ismate(d):
        return topo.mates(ch, topo.chip(T.cores[d]))

    fp = sorted([far[0:2], far[2:4]], key=lambda p: any(ismate(d) for d in p))
    cand = [h for h in range(NSIM) if h != me and topo.chip(h) == ch
            and all(topo.may_write(h, T.cores[d]) for d in far)]
    own = [h for h in cand if topo.die(h) == topo.die(me)]
    oth = [h for h in cand if h not in own]
    a = (own + oth)[0]
    b = [h for h in oth + own if h != a][0]
    return {"near": near, "far": far, "ownp": ownp, "na": na, "nb": nb, "p1": fp[0][::-1] if r % 2 else fp[0],
            "p2": sorted(fp[1], key=ismate), "hs": [a, b]}


def _off(src, dst, topo):
    return _bits(topo.mask(src, dst))


def _feed_engines(r, T, topo):
    lay = _layout(r, T, topo)
    me = T.cores[r]
    off = _off(me, T.cores[lay["near"][0]], topo)
    return [b for b in _off(me, lay["hs"][0], topo) if b not in off]


def _send(g, T, topo, items, local_sem):
    trs = []
    for dst_core, dst, src, eng, sem in items:
        rid, pid, _ = topo.addr(dst_core)
        trs.append(RemoteDMATransfer(dst_ids=[DstId(rid=rid, pnc=pid)], dma_engine_mask=_mk(eng),
                                     remote_sem=sem, src=src, dst=dst))
    g.remote_dma_fused(trs, local_sem=local_sem)
    return sum(len(it[3]) for it in items)


def _qcol(d, n):
    return slice(d * TW, (d + n) * TW)


def _helper(g, core, T, topo):
    S = T.sem
    own = [r for r in range(N) if topo.chip(T.cores[r]) == topo.chip(core)]
    if not own:
        return
    r = own[0]
    lay = _layout(r, T, topo)
    if core not in lay["hs"]:
        return
    k = lay["hs"].index(core)
    hf = len(_feed_engines(r, T, topo)) // 2
    arr = S["a%d" % r]
    n = 0
    for fed, pair in ((S.fed1, lay["p1"]), (S.fed2, lay["p2"])):
        d = pair[k]
        g.wait_ge(fed, hf)
        n += _send(g, T, topo, [(T.cores[d], T.lq[:, _qcol(r, 1)].bitcast(dt.uint8),
                                 T.xq[:, _qcol(d, 1)].bitcast(dt.uint8), _off(core, T.cores[d], topo), arr)], S.snt)
    g.wait_ge(S.fed3, hf)
    items = []
    for i, d in enumerate((lay["p1"], lay["p2"])[k]):
        off = _off(core, T.cores[d], topo)
        h = len(off) // 2
        items.append((T.cores[d], T.ls[:, _qcol(r, 1)], T.xs[:, _qcol(d, 1)], off[i * h:(i + 1) * h], arr))
    n += _send(g, T, topo, items, S.snt)
    g.wait_ge(S.snt, n)


def _arrivals(j, r, T, topo):
    lay = _layout(j, T, topo)
    if r in lay["far"]:
        noff = len(_off(lay["hs"][0], T.cores[r], topo))
        return noff + noff // 2
    noff = len(_off(T.cores[j], T.cores[r], topo))
    return 2 * noff if r == lay["nb"] else 2 * (noff // 2)


def rank_program(g, core, T, topo):
    r = T.rank_of(core)
    if r is None:
        _helper(g, core, T, topo)
        return
    S = T.sem
    sy, sc, ve, te = g.sync, g.scalar, g.vector, g.tensor
    lay = _layout(r, T, topo)
    far, p1, p2, hs, na, nb, ownp = lay["far"], lay["p1"], lay["p2"], lay["hs"], lay["na"], lay["nb"], lay["ownp"]
    h0 = min(na + ownp)
    fa = [j for j in far if r in _layout(j, T, topo)["p1"]]
    fb = sorted([j for j in far if r in _layout(j, T, topo)["p2"]], key=lambda j: -_layout(j, T, topo)["p2"].index(r))

    def bcol(d, n):
        return slice(d * TB, (d + n) * TB)

    qcol = _qcol

    sy.dma_start(T.xb[:, bcol(min(p1), 2)], T.x[:, bcol(min(p1), 2)]).then_inc(S.l1, 16)
    sy.dma_start(T.xb[:, bcol(min(p2), 2)], T.x[:, bcol(min(p2), 2)]).then_inc(S.l2, 16)
    sy.dma_start(T.xb[:, bcol(min(na), 2)], T.x[:, bcol(min(na), 2)]).then_inc(S.l3, 16)
    sy.dma_start(T.xb[:, bcol(min(ownp), 2)], T.x[:, bcol(min(ownp), 2)]).then_inc(S.l4, 16)
    sy.dma_start(T.wb[:, bcol(h0, 4)], T.w[:, bcol(h0, 4)]).then_inc(S.lw1, 16)
    sc.wait_ge(S.g1, 1)
    sc.dma_start(T.wb[:, bcol(min(fa), 2)], T.w[:, bcol(min(fa), 2)]).then_inc(S.lw2, 16)
    sc.wait_ge(S.g2, 1)
    sc.dma_start(T.wb[:, bcol(fb[0], 1)], T.w[:, bcol(fb[0], 1)]).then_inc(S.lw3, 16)
    sc.dma_start(T.wb[:, bcol(fb[1], 1)], T.w[:, bcol(fb[1], 1)]).then_inc(S.lw4, 16)

    for lsem, qsem, q, s, b, d, n in ((S.l1, S.q1, T.xq, T.xs, T.xb, min(p1), 2), (S.l2, S.q2, T.xq, T.xs, T.xb, min(p2), 2),
                                      (S.l3, S.q3, T.xq, T.xs, T.xb, min(na), 2), (S.l4, S.q4, T.xq, T.xs, T.xb, min(ownp), 2),
                                      (S.lw1, S.v1, T.wq, T.ws, T.wb, h0, 4),
                                      (S.lw2, S.v2, T.wq, T.ws, T.wb, min(fa), 2), (S.lw3, S.v3, T.wq, T.ws, T.wb, fb[0], 1),
                                      (S.lw4, S.v4, T.wq, T.ws, T.wb, fb[1], 1)):
        ve.wait_ge(lsem, 16)
        ve.quantize_mx(q[:, qcol(d, n)], s[:, qcol(d, n)], b[:, bcol(d, n)]).then_inc(qsem, 1)

    fe = _feed_engines(r, T, topo)
    hf = len(fe) // 2
    arr = S["a%d" % r]
    sent = 0
    for qsem, fed, pair in ((S.q1, S.fed1, p1), (S.q2, S.fed2, p2)):
        g.wait_ge(qsem, 1)
        sent += _send(g, T, topo, [(hs[i], T.xq[:, qcol(d, 1)].bitcast(dt.uint8), T.xq[:, qcol(d, 1)].bitcast(dt.uint8),
                                    fe[i * hf:(i + 1) * hf], fed) for i, d in enumerate(pair)], S.snt)
    sent += _send(g, T, topo, [(hs[i], T.xs[:, qcol(min(pair), 2)], T.xs[:, qcol(min(pair), 2)],
                                fe[i * hf:(i + 1) * hf], S.fed3) for i, pair in enumerate((p1, p2))], S.snt)
    g.sem_inc(S.g1, 1)
    g.wait_ge(S.q3, 1)
    off = _off(core, T.cores[na[0]], topo)
    ho = len(off) // 2
    sent += _send(g, T, topo, [(T.cores[d], T.lq[:, qcol(r, 1)].bitcast(dt.uint8), T.xq[:, qcol(d, 1)].bitcast(dt.uint8),
                                off[i * ho:(i + 1) * ho], arr) for i, d in enumerate(na)], S.snt)
    sent += _send(g, T, topo, [(T.cores[d], T.ls[:, qcol(r, 1)], T.xs[:, qcol(d, 1)],
                                off[i * ho:(i + 1) * ho], arr) for i, d in enumerate(na)], S.snt)
    g.sem_inc(S.g2, 1)
    g.wait_ge(S.q4, 1)
    sent += _send(g, T, topo, [(T.cores[nb], T.lq[:, qcol(r, 1)].bitcast(dt.uint8),
                                T.xq[:, qcol(nb, 1)].bitcast(dt.uint8), off, arr)], S.snt)
    sent += _send(g, T, topo, [(T.cores[nb], T.ls[:, qcol(r, 1)], T.xs[:, qcol(nb, 1)], off, arr)], S.snt)

    srcs = [(j, S.v1) for j in [r] + na] + [(j, S.v2) for j in fa] + [(nb, S.v1), (fb[0], S.v3), (fb[1], S.v4)]
    for i, (j, vsem) in enumerate(srcs):
        te.wait_ge(vsem, 1)
        if j == r:
            te.wait_ge(S.q4, 1)
            xc, xp = T.xq[:, qcol(r, 1)], T.xs[:, qcol(r, 1)]
        else:
            te.wait_ge(S["a%d" % j], _arrivals(j, r, T, topo))
            xc, xp = T.lq[:, qcol(j, 1)], T.ls[:, qcol(j, 1)]
        mmi = te.matmul_mx(T.ps[:, 0:128], T.wq[:, qcol(j, 1)], T.ws[:, qcol(j, 1)], xc, xp, i == 0, i == N - 1)
    mmi.then_inc(S.mm, 1)

    ve.wait_ge(S.mm, 1)
    ve.tensor_copy(T.yb[:], T.ps[:, 0:128]).then_inc(S.cp, 1)
    sy.wait_ge(S.cp, 1)
    sy.dma_start(T.y[:, :], T.yb[:]).then_inc(S.st, 16)
    sy.wait_ge(S.st, 16)
    g.wait_ge(S.snt, sent)
